import numpy as np
import ml_dtypes


def mxq(x, axis, fmt="e4m3"):
    dtype, down = {"e4m3": (ml_dtypes.float8_e4m3fn, 7), "e5m2": (ml_dtypes.float8_e5m2, 14)}[fmt]
    v = np.moveaxis(np.asarray(x, np.float32).astype(ml_dtypes.bfloat16).astype(np.float64), axis, -1)
    blocks = v.reshape(v.shape[:-1] + (-1, 32))
    amax = np.abs(blocks).max(-1, keepdims=True)
    byte = np.maximum(np.where(amax > 0, np.frexp(amax)[1] - 1 + 127, 0) - down, 1)
    scale = np.exp2(byte - 127.0)
    codes = (blocks / scale).astype(np.float32).astype(dtype).astype(np.float64)
    return np.moveaxis((codes * scale).reshape(v.shape), -1, axis)


WIDE = False


def mx_kscale(k):
    if not WIDE:
        return np.ones(k)
    levels = np.array([10, -10, 5, -5, 0])
    if k % 512:
        return np.exp2(np.random.permutation(np.resize(levels, k // 32))).repeat(32)
    a = np.empty((k // 512, 16))
    for p in range(k // 512):
        a[p, :8] = np.random.permutation(np.resize(levels, 8))
        for g in range(8):
            far = levels[np.abs(levels - a[p, g]) >= 10]
            a[p, g + 8] = far[np.random.randint(len(far))]
    return np.exp2(a.ravel()).repeat(32)


def f64(x):
    return np.asarray(x).astype(np.float64)


def striped(idx):
    return np.tile(np.asarray(idx).reshape(-1, 16).T, (8, 1)).astype(np.uint16)


def unstriped(offs):
    return offs[:16].T.reshape(-1).astype(np.int64)


E2M1 = np.array([0.0, 0.5, 1.0, 1.5, 2.0, 3.0, 4.0, 6.0, -0.0, -0.5, -1.0, -1.5, -2.0, -3.0, -4.0, -6.0])


def pack_weight(w, fmt):
    k, n = w.shape
    w = f64(np.asarray(w, np.float32).astype(ml_dtypes.bfloat16)).reshape(k // 32, 32, n)
    amax = np.abs(w).max(1)
    if fmt == "e4m3":
        byte = np.frexp(amax)[1] - 1 + 127 - 7
    else:
        mant, ex = np.frexp(amax / 6.0)
        byte = np.where(mant > 0.5, ex, ex - 1) + 127
    byte = np.clip(np.where(amax > 0, byte, 1), 1, 254)
    scaled = (w * np.exp2(127.0 - byte)[:, None, :]).reshape(k, n).astype(np.float32)
    by_word = np.ascontiguousarray(scaled.reshape(k // 512, 128, 4, n).transpose(0, 1, 3, 2))
    if fmt == "e4m3":
        words = by_word.astype(ml_dtypes.float8_e4m3fn).view(np.uint8)
    else:
        c = by_word.astype(ml_dtypes.float4_e2m1fn).view(np.uint8) & 0xF
        words = (c[..., 0::2] | (c[..., 1::2] << 4)).reshape(k // 512, 128, 2 * n)
    return np.ascontiguousarray(words), np.ascontiguousarray(byte.astype(np.uint8).reshape(k // 512, 16, n))


def unpack_weight(words, scales, fmt):
    g, _, n = scales.shape
    words = np.ascontiguousarray(words).reshape(g, 128, n, -1)
    if fmt == "e4m3":
        vals = words.view(ml_dtypes.float8_e4m3fn).astype(np.float64)
    else:
        nib = np.empty((g, 128, n, 4), np.uint8)
        nib[..., 0::2] = words & 0xF
        nib[..., 1::2] = words >> 4
        vals = E2M1[nib]
    vals = vals * np.repeat(np.exp2(scales.astype(np.float64) - 127.0), 8, axis=1)[..., None]
    return vals.transpose(0, 1, 3, 2).reshape(g * 512, n)


D, E, T, I, G, U, Q = 512, 512, 4096, 1024, 64, 512, 128


def setup_inputs():
    n = np.random.standard_normal
    idx = np.random.permutation(T)[:I]
    idx2 = np.random.permutation(U)[:G]
    fd = mx_kscale(D)
    fe = mx_kscale(E)
    keysp = pack_weight(n((D, T)) / fd[:, None], "e2m1")
    valsp = pack_weight(n((E, T)) / fe[:, None], "e2m1")
    return {
        "query": (n((D, Q)) * 0.5 / np.sqrt(D) * fd[:, None]).astype(np.float32),
        "keys_words": keysp[0],
        "keys_scales": keysp[1],
        "gout": (n((E, Q)) * 1 / np.sqrt(E) * fe[:, None]).astype(np.float32),
        "vals_words": valsp[0],
        "vals_scales": valsp[1],
        "lse": (np.random.uniform(6.8, 7.2, (Q, 1))).astype(np.float32),
        "delta": (np.random.uniform(-0.3, 0.3, (Q, 1))).astype(np.float32),
        "prior": (0.4 * n((Q, U))).astype(np.float32),
        "trust": (np.random.uniform(0.5, 1.2, (Q, 1))).astype(np.float32),
        "old": (4.0 * n((Q, U))).astype(np.float32),
        "offs": striped(idx),
        "offs2": striped(idx2),
    }


def reference(query, keys_words, keys_scales, gout, vals_words, vals_scales, lse, delta, prior, trust, old, offs, offs2):
    idx = unstriped(offs)
    idx2 = unstriped(offs2)
    keysu = unpack_weight(keys_words, keys_scales, "e2m1")
    valsu = unpack_weight(vals_words, vals_scales, "e2m1")
    queryq = mxq(f64(query), 0, "e4m3")
    keysidxg = keysu[:, idx]
    a = queryq.T @ keysidxg
    b = f64(prior)[:, idx2] * f64(trust)
    br = np.repeat(b, I // G, axis=1)
    goutq = mxq(f64(gout), 0, "e4m3")
    valsidxg = valsu[:, idx]
    dp = goutq.T @ valsidxg
    ds = np.exp(a + br - f64(lse)) * (dp - f64(delta)) * 512.0
    gb = ds.reshape(Q, G, I // G).sum(axis=2) * f64(trust)
    gf = np.zeros((Q, U))
    gf[:, idx2] = gb
    y = f64(old) + gf
    return y

@@ -1,0 +1,159 @@
+from contextlib import ExitStack
+
+import concourse.mybir as mybir
+
+D, E, T, I, G, U, Q = 512, 512, 4096, 1024, 64, 512, 128
+FLOPS = 2 * D * Q * I + 2 * E * Q * I
+
+F32 = mybir.dt.float32
+BF16 = mybir.dt.bfloat16
+I32 = mybir.dt.int32
+U32 = mybir.dt.uint32
+U16 = mybir.dt.uint16
+U8 = mybir.dt.uint8
+FP8X4 = mybir.dt.float8_e4m3fn_x4
+FP4X4 = mybir.dt.float4_e2m1fn_x4
+ALU = mybir.AluOpType
+ACT = mybir.ActivationFunctionType
+
+P = 128
+PACK = 4
+PAGE = I // G
+HALF = I // 2
+SPREAD = P // 16
+
+
+def tile_attend_gpagebias_kernel(tc, query, keys_words, keys_scales, gout, vals_words, vals_scales,
+                                  lse, delta, prior, trust, old, offs, offs2, out):
+    nc = tc.nc
+    with ExitStack() as ctx:
+        sb = ctx.enter_context(tc.tile_pool(name="sb", bufs=1))
+        ps = ctx.enter_context(tc.psum_pool(name="ps", bufs=1))
+
+        def tile(name, shape, dtype, slot=None):
+            return sb.tile(shape, dtype, name=name, tag=slot or name, align_bytes=64)
+
+        slots = sb.tile([P, I // 16], U16, name="slots")
+        pages = sb.tile([P, G // 16], U16, name="pages")
+        k_words = tile("k_words", [P, T], U16)
+        k_bytes = tile("k_bytes", [P, T], U8)
+        v_bytes = tile("v_bytes", [P, T], U8)
+        k_plane = tile("k_plane", [P, I], U8)
+        v_plane = tile("v_plane", [P, I], U8)
+        q_raw = tile("q_raw", [P, PACK, Q], F32)
+        prior_sb = tile("prior_sb", [P, U], F32)
+        lse_sb = tile("lse_sb", [P, 1], F32)
+        delta_sb = tile("delta_sb", [P, 1], F32)
+        trust_sb = tile("trust_sb", [P, 1], F32)
+        fresh = tile("fresh", [P, U], F32)
+        loss = tile("loss", [P, G], F32)
+
+        nc.vector.memset(k_bytes[:].bitcast(I32), 0)
+        nc.vector.memset(v_bytes[:].bitcast(I32), 0)
+        nc.vector.memset(k_plane[:].bitcast(I32), 0)
+        nc.vector.memset(v_plane[:].bitcast(I32), 0)
+        nc.vector.memset(fresh[:], 0.0)
+        nc.vector.memset(loss[:], 512.0)
+
+        nc.sync.dma_start(slots[:], offs)
+        nc.sync.dma_start(pages[:], offs2)
+        nc.sync.dma_start(out=k_bytes[0:P:SPREAD, :].bitcast(I32), in_=keys_scales[0].bitcast(I32))
+        nc.sync.dma_start(out=v_bytes[0:P:SPREAD, :].bitcast(I32), in_=vals_scales[0].bitcast(I32))
+        nc.scalar.dma_start(out=q_raw[:], in_=query.rearrange("(p j) q -> p j q", j=PACK))
+        nc.scalar.dma_start(out=k_words[:].bitcast(I32), in_=keys_words[0].bitcast(I32))
+        nc.scalar.dma_start(out=prior_sb[:], in_=prior)
+        nc.scalar.dma_start(out=trust_sb[:], in_=trust)
+        nc.scalar.dma_start(out=lse_sb[:], in_=lse)
+        nc.gpsimd.dma_start(out=delta_sb[:], in_=delta)
+
+        def gather_scales(name, window, plane, slot=None):
+            picked = tile(name, [P, I], U8, slot)
+            nc.vector.tensor_copy(out=picked[:], in_=window[:].indirect(slots[:]))
+            for quad in range(0, P, 32):
+                nc.sync.dma_start(out=plane[quad:quad + 4, :].bitcast(I32),
+                                  in_=picked[quad:quad + 32:SPREAD, :].bitcast(I32))
+
+        def interleave(name, raw):
+            grouped = tile(name, [P, Q, PACK], BF16)
+            nc.scalar.copy(out=grouped[:], in_=raw[:].rearrange("p j q -> p q j"))
+            return grouped
+
+        def quantize(name, grouped, slot=None):
+            codes = tile(name + "_codes", [P, Q], U32, slot)
+            scales = tile(name + "_scales", [P, Q], U8)
+            nc.vector.quantize_mx(out=codes[:].bitcast(FP8X4), scales=scales[:],
+                                  in_=grouped[:].rearrange("p q j -> p (q j)"))
+            return codes, scales
+
+        def gather_words(name, window, h, slot=None):
+            picked = tile(name, [P, HALF], U16, slot)
+            nc.vector.tensor_copy(
+                out=picked[:], in_=window[:].indirect(slots[:, h * HALF // 16:(h + 1) * HALF // 16]))
+            return picked
+
+        def product(name, rows, picked, plane, h):
+            acc = ps.tile([P, HALF], F32, name=name)
+            nc.tensor.matmul_mx(out=acc[:], lhsT=rows[0][:].bitcast(FP8X4), lhsT_scale=rows[1][:],
+                                rhs=picked[:].bitcast(FP4X4), rhs_scale=plane[:, h * HALF:(h + 1) * HALF],
+                                start=True, stop=True)
+            return acc
+
+        def weights(name, acc, bias, h, slot=None):
+            w = tile(name, [P, HALF], F32, slot)
+            for g in range(G // 2):
+                page = h * G // 2 + g
+                nc.scalar.activation(out=w[:, g * PAGE:(g + 1) * PAGE], in_=acc[:, g * PAGE:(g + 1) * PAGE],
+                                     func=ACT.Exp, bias=bias[:, page:page + 1])
+            return w
+
+        q_grouped = interleave("q_grouped", q_raw)
+        g_raw = tile("g_raw", [P, PACK, Q], F32, "q_raw")
+        nc.scalar.dma_start(out=g_raw[:], in_=gout.rearrange("(p j) q -> p j q", j=PACK))
+        gather_scales("k_picked", k_bytes, k_plane)
+        q_mx = quantize("q", q_grouped, "k_bytes")
+        v_words = tile("v_words", [P, T], U16, "q_grouped")
+        nc.sync.dma_start(out=v_words[:].bitcast(I32), in_=vals_words[0].bitcast(I32))
+        kw0 = gather_words("kw0", k_words, 0)
+        a0 = product("a0", q_mx, kw0, k_plane, 0)
+
+        neg_lse = tile("neg_lse", [P, 1], F32)
+        nc.scalar.mul(neg_lse[:], lse_sb[:], -1.0)
+        factor = tile("factor", [P, G], F32)
+        nc.scalar.activation(out=factor[:], in_=loss[:], func=ACT.Copy, scale=trust_sb[:])
+        picked_prior = tile("picked_prior", [P, G], F32)
+        nc.vector.tensor_copy(out=picked_prior[:], in_=prior_sb[:].indirect(pages[:]))
+        bias = tile("bias", [P, G], F32)
+        nc.scalar.activation(out=bias[:], in_=picked_prior[:], func=ACT.Identity, scale=trust_sb[:],
+                             bias=neg_lse[:])
+
+        g_grouped = interleave("g_grouped", g_raw)
+        w0 = weights("w0", a0, bias, 0, "q_raw")
+        gather_scales("v_picked", v_bytes, v_plane, "prior_sb")
+        kw1 = gather_words("kw1", k_words, 1, "v_bytes")
+        a1 = product("a1", q_mx, kw1, k_plane, 1)
+        w1 = weights("w1", a1, bias, 1)
+        old_sb = tile("old_sb", [P, U], F32, "k_words")
+        nc.sync.dma_start(out=old_sb[:], in_=old)
+        g_mx = quantize("g", g_grouped)
+        vw0 = gather_words("vw0", v_words, 0, "g_grouped")
+        dp0 = product("dp0", g_mx, vw0, v_plane, 0)
+        vw1 = gather_words("vw1", v_words, 1)
+        dp1 = product("dp1", g_mx, vw1, v_plane, 1)
+
+        ds = []
+        for h, (dp, w) in enumerate(((dp0, w0), (dp1, w1))):
+            d = tile("ds%d" % h, [P, HALF], F32)
+            nc.vector.scalar_tensor_tensor(out=d[:], in0=dp[:], scalar=delta_sb[:], in1=w[:],
+                                           op0=ALU.subtract, op1=ALU.mult)
+            ds.append(d)
+        sums = tile("sums", [P, G], F32, "w1")
+        for h in range(2):
+            nc.vector.tensor_reduce(out=sums[:, h * G // 2:(h + 1) * G // 2],
+                                    in_=ds[h][:].rearrange("p (g j) -> p g j", j=PAGE),
+                                    axis=mybir.AxisListType.X, op=ALU.add)
+        nc.vector.tensor_tensor(out=fresh[:].indirect(pages[:]), in0=sums[:], in1=factor[:], op=ALU.mult)
+        for c, queue in enumerate((nc.sync, nc.scalar)):
+            cols = slice(c * U // 2, (c + 1) * U // 2)
+            result = tile("result%d" % c, [P, U // 2], F32)
+            nc.vector.tensor_tensor(out=result[:], in0=old_sb[:, cols], in1=fresh[:, cols], op=ALU.add)
+            queue.dma_start(out=out[:, cols], in_=result[:])

@@ -20,7 +20,6 @@ P = 128
 PACK = 4
 PAGE = I // G
 HALF = I // 2
-SPREAD = P // 16
 
 
 def tile_attend_gpagebias_kernel(tc, query, keys_words, keys_scales, gout, vals_words, vals_scales,
@@ -38,8 +37,6 @@ def tile_attend_gpagebias_kernel(tc, query, keys_words, keys_scales, gout, vals_
         k_words = tile("k_words", [P, T], U16)
         k_bytes = tile("k_bytes", [P, T], U8)
         v_bytes = tile("v_bytes", [P, T], U8)
-        k_plane = tile("k_plane", [P, I], U8)
-        v_plane = tile("v_plane", [P, I], U8)
         q_raw = tile("q_raw", [P, PACK, Q], F32)
         prior_sb = tile("prior_sb", [P, U], F32)
         lse_sb = tile("lse_sb", [P, 1], F32)
@@ -48,30 +45,38 @@ def tile_attend_gpagebias_kernel(tc, query, keys_words, keys_scales, gout, vals_
         fresh = tile("fresh", [P, U], F32)
         loss = tile("loss", [P, G], F32)
 
+        ones = tile("ones", [P, G], F32)
+        nc.gpsimd.memset(ones[:], 1.0)
+        nc.scalar.mul(loss[:], ones[:], 512.0)
         nc.vector.memset(k_bytes[:].bitcast(I32), 0)
         nc.vector.memset(v_bytes[:].bitcast(I32), 0)
-        nc.vector.memset(k_plane[:].bitcast(I32), 0)
-        nc.vector.memset(v_plane[:].bitcast(I32), 0)
         nc.vector.memset(fresh[:], 0.0)
-        nc.vector.memset(loss[:], 512.0)
+
+        def load_scales(window, rows):
+            for quad in range(4):
+                nc.sync.dma_start(out=window[32 * quad:32 * quad + 4, :].bitcast(I32),
+                                  in_=rows[0, 4 * quad:4 * quad + 4, :].bitcast(I32))
 
         nc.sync.dma_start(slots[:], offs)
+        nc.sync.dma_start(out=k_words[:].bitcast(I32), in_=keys_words[0].bitcast(I32))
+        nc.sync.dma_start(out=q_raw[:], in_=query.rearrange("(p j) q -> p j q", j=PACK))
+        load_scales(k_bytes, keys_scales)
+        nc.sync.dma_start(out=prior_sb[:], in_=prior)
         nc.sync.dma_start(pages[:], offs2)
-        nc.sync.dma_start(out=k_bytes[0:P:SPREAD, :].bitcast(I32), in_=keys_scales[0].bitcast(I32))
-        nc.sync.dma_start(out=v_bytes[0:P:SPREAD, :].bitcast(I32), in_=vals_scales[0].bitcast(I32))
-        nc.scalar.dma_start(out=q_raw[:], in_=query.rearrange("(p j) q -> p j q", j=PACK))
-        nc.scalar.dma_start(out=k_words[:].bitcast(I32), in_=keys_words[0].bitcast(I32))
-        nc.scalar.dma_start(out=prior_sb[:], in_=prior)
-        nc.scalar.dma_start(out=trust_sb[:], in_=trust)
-        nc.scalar.dma_start(out=lse_sb[:], in_=lse)
+        load_scales(v_bytes, vals_scales)
+        g_raw = tile("g_raw", [P, PACK, Q], F32)
+        nc.sync.dma_start(out=g_raw[:], in_=gout.rearrange("(p j) q -> p j q", j=PACK))
+        v_words = tile("v_words", [P, T], U16)
+        nc.sync.dma_start(out=v_words[:].bitcast(I32), in_=vals_words[0].bitcast(I32))
+        nc.gpsimd.dma_start(out=trust_sb[:], in_=trust)
+        nc.gpsimd.dma_start(out=lse_sb[:], in_=lse)
         nc.gpsimd.dma_start(out=delta_sb[:], in_=delta)
 
-        def gather_scales(name, window, plane, slot=None):
-            picked = tile(name, [P, I], U8, slot)
-            nc.vector.tensor_copy(out=picked[:], in_=window[:].indirect(slots[:]))
-            for quad in range(0, P, 32):
-                nc.sync.dma_start(out=plane[quad:quad + 4, :].bitcast(I32),
-                                  in_=picked[quad:quad + 32:SPREAD, :].bitcast(I32))
+        def gather(name, window, dtype, first, count, slot=None):
+            picked = tile(name, [P, count], dtype, slot)
+            nc.vector.tensor_copy(
+                out=picked[:], in_=window[:].indirect(slots[:, first // 16:(first + count) // 16]))
+            return picked
 
         def interleave(name, raw):
             grouped = tile(name, [P, Q, PACK], BF16)
@@ -85,36 +90,23 @@ def tile_attend_gpagebias_kernel(tc, query, keys_words, keys_scales, gout, vals_
                                   in_=grouped[:].rearrange("p q j -> p (q j)"))
             return codes, scales
 
-        def gather_words(name, window, h, slot=None):
-            picked = tile(name, [P, HALF], U16, slot)
-            nc.vector.tensor_copy(
-                out=picked[:], in_=window[:].indirect(slots[:, h * HALF // 16:(h + 1) * HALF // 16]))
-            return picked
-
-        def product(name, rows, picked, plane, h):
+        def product(name, rows, words, scales):
             acc = ps.tile([P, HALF], F32, name=name)
             nc.tensor.matmul_mx(out=acc[:], lhsT=rows[0][:].bitcast(FP8X4), lhsT_scale=rows[1][:],
-                                rhs=picked[:].bitcast(FP4X4), rhs_scale=plane[:, h * HALF:(h + 1) * HALF],
-                                start=True, stop=True)
+                                rhs=words.bitcast(FP4X4), rhs_scale=scales, start=True, stop=True)
             return acc
 
-        def weights(name, acc, bias, h, slot=None):
-            w = tile(name, [P, HALF], F32, slot)
+        def weights(w, acc, bias, h):
             for g in range(G // 2):
                 page = h * G // 2 + g
-                nc.scalar.activation(out=w[:, g * PAGE:(g + 1) * PAGE], in_=acc[:, g * PAGE:(g + 1) * PAGE],
+                nc.scalar.activation(out=w[:, page * PAGE:(page + 1) * PAGE], in_=acc[:, g * PAGE:(g + 1) * PAGE],
                                      func=ACT.Exp, bias=bias[:, page:page + 1])
-            return w
 
+        kw = gather("kw", k_words, U16, 0, I)
         q_grouped = interleave("q_grouped", q_raw)
-        g_raw = tile("g_raw", [P, PACK, Q], F32, "q_raw")
-        nc.scalar.dma_start(out=g_raw[:], in_=gout.rearrange("(p j) q -> p j q", j=PACK))
-        gather_scales("k_picked", k_bytes, k_plane)
-        q_mx = quantize("q", q_grouped, "k_bytes")
-        v_words = tile("v_words", [P, T], U16, "q_grouped")
-        nc.sync.dma_start(out=v_words[:].bitcast(I32), in_=vals_words[0].bitcast(I32))
-        kw0 = gather_words("kw0", k_words, 0)
-        a0 = product("a0", q_mx, kw0, k_plane, 0)
+        q_mx = quantize("q", q_grouped)
+        ks0 = gather("ks0", k_bytes, U8, 0, HALF)
+        a0 = product("a0", q_mx, kw[:, :HALF], ks0[:])
 
         neg_lse = tile("neg_lse", [P, 1], F32)
         nc.scalar.mul(neg_lse[:], lse_sb[:], -1.0)
@@ -127,26 +119,28 @@ def tile_attend_gpagebias_kernel(tc, query, keys_words, keys_scales, gout, vals_
                              bias=neg_lse[:])
 
         g_grouped = interleave("g_grouped", g_raw)
-        w0 = weights("w0", a0, bias, 0, "q_raw")
-        gather_scales("v_picked", v_bytes, v_plane, "prior_sb")
-        kw1 = gather_words("kw1", k_words, 1, "v_bytes")
-        a1 = product("a1", q_mx, kw1, k_plane, 1)
-        w1 = weights("w1", a1, bias, 1)
-        old_sb = tile("old_sb", [P, U], F32, "k_words")
+        w = tile("w", [P, I], F32, "g_raw")
+        weights(w, a0, bias, 0)
+        ks1 = gather("ks1", k_bytes, U8, HALF, HALF)
+        a1 = product("a1", q_mx, kw[:, HALF:], ks1[:])
+        old_sb = tile("old_sb", [P, U], F32, "kw")
         nc.sync.dma_start(out=old_sb[:], in_=old)
+        weights(w, a1, bias, 1)
+        vs = gather("vs", v_bytes, U8, 0, I)
         g_mx = quantize("g", g_grouped)
-        vw0 = gather_words("vw0", v_words, 0, "g_grouped")
-        dp0 = product("dp0", g_mx, vw0, v_plane, 0)
-        vw1 = gather_words("vw1", v_words, 1)
-        dp1 = product("dp1", g_mx, vw1, v_plane, 1)
+        vw = tile("vw", [P, I], U16)
+        nc.vector.tensor_copy(out=vw[:, :HALF], in_=v_words[:].indirect(slots[:, :HALF // 16]))
+        dp0 = product("dp0", g_mx, vw[:, :HALF], vs[:, :HALF])
+        nc.vector.tensor_copy(out=vw[:, HALF:], in_=v_words[:].indirect(slots[:, HALF // 16:]))
+        dp1 = product("dp1", g_mx, vw[:, HALF:], vs[:, HALF:])
 
         ds = []
-        for h, (dp, w) in enumerate(((dp0, w0), (dp1, w1))):
+        for h, dp in enumerate((dp0, dp1)):
             d = tile("ds%d" % h, [P, HALF], F32)
-            nc.vector.scalar_tensor_tensor(out=d[:], in0=dp[:], scalar=delta_sb[:], in1=w[:],
+            nc.vector.scalar_tensor_tensor(out=d[:], in0=dp[:], scalar=delta_sb[:], in1=w[:, h * HALF:(h + 1) * HALF],
                                            op0=ALU.subtract, op1=ALU.mult)
             ds.append(d)
-        sums = tile("sums", [P, G], F32, "w1")
+        sums = tile("sums", [P, G], F32, "g_raw")
         for h in range(2):
             nc.vector.tensor_reduce(out=sums[:, h * G // 2:(h + 1) * G // 2],
                                     in_=ds[h][:].rearrange("p (g j) -> p g j", j=PAGE),

@@ -20,6 +20,7 @@ P = 128
 PACK = 4
 PAGE = I // G
 HALF = I // 2
+SPREAD = P // 16
 
 
 def tile_attend_gpagebias_kernel(tc, query, keys_words, keys_scales, gout, vals_words, vals_scales,
@@ -45,32 +46,36 @@ def tile_attend_gpagebias_kernel(tc, query, keys_words, keys_scales, gout, vals_
         fresh = tile("fresh", [P, U], F32)
         loss = tile("loss", [P, G], F32)
 
+        k_plane = tile("k_plane", [P, I], U8)
+        v_plane = tile("v_plane", [P, I], U8)
+        g_raw = tile("g_raw", [P, PACK, Q], F32)
+        v_words = tile("v_words", [P, T], U16)
         ones = tile("ones", [P, G], F32)
-        nc.gpsimd.memset(ones[:], 1.0)
-        nc.scalar.mul(loss[:], ones[:], 512.0)
         nc.vector.memset(k_bytes[:].bitcast(I32), 0)
         nc.vector.memset(v_bytes[:].bitcast(I32), 0)
+        nc.vector.memset(ones[:], 1.0)
+        nc.vector.memset(k_plane[:].bitcast(I32), 0)
+        nc.vector.memset(v_plane[:].bitcast(I32), 0)
         nc.vector.memset(fresh[:], 0.0)
-
-        def load_scales(window, rows):
-            for quad in range(4):
-                nc.sync.dma_start(out=window[32 * quad:32 * quad + 4, :].bitcast(I32),
-                                  in_=rows[0, 4 * quad:4 * quad + 4, :].bitcast(I32))
 
         nc.sync.dma_start(slots[:], offs)
         nc.sync.dma_start(out=k_words[:].bitcast(I32), in_=keys_words[0].bitcast(I32))
-        nc.sync.dma_start(out=q_raw[:], in_=query.rearrange("(p j) q -> p j q", j=PACK))
-        load_scales(k_bytes, keys_scales)
         nc.sync.dma_start(out=prior_sb[:], in_=prior)
+        nc.sync.dma_start(out=q_raw[:], in_=query.rearrange("(p j) q -> p j q", j=PACK))
         nc.sync.dma_start(pages[:], offs2)
-        load_scales(v_bytes, vals_scales)
-        g_raw = tile("g_raw", [P, PACK, Q], F32)
         nc.sync.dma_start(out=g_raw[:], in_=gout.rearrange("(p j) q -> p j q", j=PACK))
-        v_words = tile("v_words", [P, T], U16)
         nc.sync.dma_start(out=v_words[:].bitcast(I32), in_=vals_words[0].bitcast(I32))
-        nc.gpsimd.dma_start(out=trust_sb[:], in_=trust)
-        nc.gpsimd.dma_start(out=lse_sb[:], in_=lse)
-        nc.gpsimd.dma_start(out=delta_sb[:], in_=delta)
+        nc.scalar.dma_start(out=trust_sb[:], in_=trust)
+        nc.scalar.dma_start(out=lse_sb[:], in_=lse)
+        nc.scalar.dma_start(out=delta_sb[:], in_=delta)
+        nc.scalar.dma_start(out=k_bytes[0:P:SPREAD, :].bitcast(I32), in_=keys_scales[0].bitcast(I32))
+        nc.scalar.dma_start(out=v_bytes[0:P:SPREAD, :].bitcast(I32), in_=vals_scales[0].bitcast(I32))
+        nc.scalar.mul(loss[:], ones[:], 512.0)
+
+        def to_plane(picked, plane):
+            for quad in range(0, P, 32):
+                nc.sync.dma_start(out=plane[quad:quad + 4, :].bitcast(I32),
+                                  in_=picked[quad:quad + 32:SPREAD, :].bitcast(I32))
 
         def gather(name, window, dtype, first, count, slot=None):
             picked = tile(name, [P, count], dtype, slot)
@@ -102,37 +107,36 @@ def tile_attend_gpagebias_kernel(tc, query, keys_words, keys_scales, gout, vals_
                 nc.scalar.activation(out=w[:, page * PAGE:(page + 1) * PAGE], in_=acc[:, g * PAGE:(g + 1) * PAGE],
                                      func=ACT.Exp, bias=bias[:, page:page + 1])
 
-        kw = gather("kw", k_words, U16, 0, I)
+        to_plane(gather("ks", k_bytes, U8, 0, I), k_plane)
+        kw0 = gather("kw0", k_words, U16, 0, HALF, "k_bytes")
+        picked_prior = tile("picked_prior", [P, G], F32)
+        nc.vector.tensor_copy(out=picked_prior[:], in_=prior_sb[:].indirect(pages[:]))
         q_grouped = interleave("q_grouped", q_raw)
         q_mx = quantize("q", q_grouped)
-        ks0 = gather("ks0", k_bytes, U8, 0, HALF)
-        a0 = product("a0", q_mx, kw[:, :HALF], ks0[:])
+        a0 = product("a0", q_mx, kw0[:], k_plane[:, :HALF])
 
         neg_lse = tile("neg_lse", [P, 1], F32)
         nc.scalar.mul(neg_lse[:], lse_sb[:], -1.0)
         factor = tile("factor", [P, G], F32)
         nc.scalar.activation(out=factor[:], in_=loss[:], func=ACT.Copy, scale=trust_sb[:])
-        picked_prior = tile("picked_prior", [P, G], F32)
-        nc.vector.tensor_copy(out=picked_prior[:], in_=prior_sb[:].indirect(pages[:]))
         bias = tile("bias", [P, G], F32)
         nc.scalar.activation(out=bias[:], in_=picked_prior[:], func=ACT.Identity, scale=trust_sb[:],
                              bias=neg_lse[:])
-
         g_grouped = interleave("g_grouped", g_raw)
-        w = tile("w", [P, I], F32, "g_raw")
+        w = tile("w", [P, I], F32)
         weights(w, a0, bias, 0)
-        ks1 = gather("ks1", k_bytes, U8, HALF, HALF)
-        a1 = product("a1", q_mx, kw[:, HALF:], ks1[:])
-        old_sb = tile("old_sb", [P, U], F32, "kw")
-        nc.sync.dma_start(out=old_sb[:], in_=old)
-        weights(w, a1, bias, 1)
-        vs = gather("vs", v_bytes, U8, 0, I)
+
+        to_plane(gather("vs", v_bytes, U8, 0, I, "q_raw"), v_plane)
         g_mx = quantize("g", g_grouped)
-        vw = tile("vw", [P, I], U16)
-        nc.vector.tensor_copy(out=vw[:, :HALF], in_=v_words[:].indirect(slots[:, :HALF // 16]))
-        dp0 = product("dp0", g_mx, vw[:, :HALF], vs[:, :HALF])
-        nc.vector.tensor_copy(out=vw[:, HALF:], in_=v_words[:].indirect(slots[:, HALF // 16:]))
-        dp1 = product("dp1", g_mx, vw[:, HALF:], vs[:, HALF:])
+        kw1 = gather("kw1", k_words, U16, HALF, HALF, "g_raw")
+        a1 = product("a1", q_mx, kw1[:], k_plane[:, HALF:])
+        weights(w, a1, bias, 1)
+        old_sb = tile("old_sb", [P, U], F32, "k_words")
+        nc.sync.dma_start(out=old_sb[:], in_=old)
+        vw0 = gather("vw0", v_words, U16, 0, HALF)
+        dp0 = product("dp0", g_mx, vw0[:], v_plane[:, :HALF])
+        vw1 = gather("vw1", v_words, U16, HALF, HALF)
+        dp1 = product("dp1", g_mx, vw1[:], v_plane[:, HALF:])
 
         ds = []
         for h, dp in enumerate((dp0, dp1)):
@@ -140,7 +144,7 @@ def tile_attend_gpagebias_kernel(tc, query, keys_words, keys_scales, gout, vals_
             nc.vector.scalar_tensor_tensor(out=d[:], in0=dp[:], scalar=delta_sb[:], in1=w[:, h * HALF:(h + 1) * HALF],
                                            op0=ALU.subtract, op1=ALU.mult)
             ds.append(d)
-        sums = tile("sums", [P, G], F32, "g_raw")
+        sums = tile("sums", [P, G], F32, "w")
         for h in range(2):
             nc.vector.tensor_reduce(out=sums[:, h * G // 2:(h + 1) * G // 2],
                                     in_=ds[h][:].rearrange("p (g j) -> p g j", j=PAGE),

@@ -51,26 +51,26 @@ def tile_attend_gpagebias_kernel(tc, query, keys_words, keys_scales, gout, vals_
         g_raw = tile("g_raw", [P, PACK, Q], F32)
         v_words = tile("v_words", [P, T], U16)
         ones = tile("ones", [P, G], F32)
+        nc.gpsimd.memset(ones[:], 1.0)
+        nc.scalar.mul(loss[:], ones[:], 512.0)
         nc.vector.memset(k_bytes[:].bitcast(I32), 0)
         nc.vector.memset(v_bytes[:].bitcast(I32), 0)
-        nc.vector.memset(ones[:], 1.0)
         nc.vector.memset(k_plane[:].bitcast(I32), 0)
         nc.vector.memset(v_plane[:].bitcast(I32), 0)
         nc.vector.memset(fresh[:], 0.0)
 
         nc.sync.dma_start(slots[:], offs)
-        nc.sync.dma_start(out=k_words[:].bitcast(I32), in_=keys_words[0].bitcast(I32))
-        nc.sync.dma_start(out=prior_sb[:], in_=prior)
         nc.sync.dma_start(out=q_raw[:], in_=query.rearrange("(p j) q -> p j q", j=PACK))
+        nc.sync.dma_start(out=prior_sb[:], in_=prior)
+        nc.sync.dma_start(out=k_bytes[0:P:SPREAD, :].bitcast(I32), in_=keys_scales[0].bitcast(I32))
+        nc.sync.dma_start(out=k_words[:].bitcast(I32), in_=keys_words[0].bitcast(I32))
         nc.sync.dma_start(pages[:], offs2)
+        nc.sync.dma_start(out=trust_sb[:], in_=trust)
+        nc.sync.dma_start(out=lse_sb[:], in_=lse)
+        nc.sync.dma_start(out=v_bytes[0:P:SPREAD, :].bitcast(I32), in_=vals_scales[0].bitcast(I32))
         nc.sync.dma_start(out=g_raw[:], in_=gout.rearrange("(p j) q -> p j q", j=PACK))
         nc.sync.dma_start(out=v_words[:].bitcast(I32), in_=vals_words[0].bitcast(I32))
-        nc.scalar.dma_start(out=trust_sb[:], in_=trust)
-        nc.scalar.dma_start(out=lse_sb[:], in_=lse)
-        nc.scalar.dma_start(out=delta_sb[:], in_=delta)
-        nc.scalar.dma_start(out=k_bytes[0:P:SPREAD, :].bitcast(I32), in_=keys_scales[0].bitcast(I32))
-        nc.scalar.dma_start(out=v_bytes[0:P:SPREAD, :].bitcast(I32), in_=vals_scales[0].bitcast(I32))
-        nc.scalar.mul(loss[:], ones[:], 512.0)
+        nc.sync.dma_start(out=delta_sb[:], in_=delta)
 
         def to_plane(picked, plane):
             for quad in range(0, P, 32):
@@ -107,12 +107,13 @@ def tile_attend_gpagebias_kernel(tc, query, keys_words, keys_scales, gout, vals_
                 nc.scalar.activation(out=w[:, page * PAGE:(page + 1) * PAGE], in_=acc[:, g * PAGE:(g + 1) * PAGE],
                                      func=ACT.Exp, bias=bias[:, page:page + 1])
 
-        to_plane(gather("ks", k_bytes, U8, 0, I), k_plane)
-        kw0 = gather("kw0", k_words, U16, 0, HALF, "k_bytes")
-        picked_prior = tile("picked_prior", [P, G], F32)
-        nc.vector.tensor_copy(out=picked_prior[:], in_=prior_sb[:].indirect(pages[:]))
         q_grouped = interleave("q_grouped", q_raw)
         q_mx = quantize("q", q_grouped)
+        ks = gather("ks", k_bytes, U8, 0, I)
+        to_plane(ks, k_plane)
+        kw0 = gather("kw0", k_words, U16, 0, HALF)
+        picked_prior = tile("picked_prior", [P, G], F32)
+        nc.vector.tensor_copy(out=picked_prior[:], in_=prior_sb[:].indirect(pages[:]))
         a0 = product("a0", q_mx, kw0[:], k_plane[:, :HALF])
 
         neg_lse = tile("neg_lse", [P, 1], F32)
@@ -126,7 +127,7 @@ def tile_attend_gpagebias_kernel(tc, query, keys_words, keys_scales, gout, vals_
         w = tile("w", [P, I], F32)
         weights(w, a0, bias, 0)
 
-        to_plane(gather("vs", v_bytes, U8, 0, I, "q_raw"), v_plane)
+        to_plane(gather("vs", v_bytes, U8, 0, I), v_plane)
         g_mx = quantize("g", g_grouped)
         kw1 = gather("kw1", k_words, U16, HALF, HALF, "g_raw")
         a1 = product("a1", q_mx, kw1[:], k_plane[:, HALF:])

@@ -18,9 +18,13 @@ ACT = mybir.ActivationFunctionType
 
 P = 128
 PACK = 4
+QUADRANT = 32
+QUADRANT_BLOCKS = 4
+SPREAD = QUADRANT // QUADRANT_BLOCKS
+LIST_ROWS = 16
 PAGE = I // G
 HALF = I // 2
-SPREAD = P // 16
+LOSS_SCALE = 512.0
 
 
 def tile_attend_gpagebias_kernel(tc, query, keys_words, keys_scales, gout, vals_words, vals_scales,
@@ -30,11 +34,11 @@ def tile_attend_gpagebias_kernel(tc, query, keys_words, keys_scales, gout, vals_
         sb = ctx.enter_context(tc.tile_pool(name="sb", bufs=1))
         ps = ctx.enter_context(tc.psum_pool(name="ps", bufs=1))
 
-        def tile(name, shape, dtype, slot=None):
-            return sb.tile(shape, dtype, name=name, tag=slot or name, align_bytes=64)
+        def tile(name, shape, dtype, reuse=None):
+            return sb.tile(shape, dtype, name=name, tag=reuse or name, align_bytes=64)
 
-        slots = sb.tile([P, I // 16], U16, name="slots")
-        pages = sb.tile([P, G // 16], U16, name="pages")
+        slots = sb.tile([P, I // LIST_ROWS], U16, name="slots")
+        pages = sb.tile([P, G // LIST_ROWS], U16, name="pages")
         k_words = tile("k_words", [P, T], U16)
         k_bytes = tile("k_bytes", [P, T], U8)
         v_bytes = tile("v_bytes", [P, T], U8)
@@ -45,14 +49,15 @@ def tile_attend_gpagebias_kernel(tc, query, keys_words, keys_scales, gout, vals_
         trust_sb = tile("trust_sb", [P, 1], F32)
         fresh = tile("fresh", [P, U], F32)
         loss = tile("loss", [P, G], F32)
-
         k_plane = tile("k_plane", [P, I], U8)
         v_plane = tile("v_plane", [P, I], U8)
         g_raw = tile("g_raw", [P, PACK, Q], F32)
         v_words = tile("v_words", [P, T], U16)
         ones = tile("ones", [P, G], F32)
+
         nc.gpsimd.memset(ones[:], 1.0)
-        nc.scalar.mul(loss[:], ones[:], 512.0)
+        nc.scalar.mul(loss[:], ones[:], LOSS_SCALE)
+
         nc.vector.memset(k_bytes[:].bitcast(I32), 0)
         nc.vector.memset(v_bytes[:].bitcast(I32), 0)
         nc.vector.memset(k_plane[:].bitcast(I32), 0)
@@ -72,49 +77,50 @@ def tile_attend_gpagebias_kernel(tc, query, keys_words, keys_scales, gout, vals_
         nc.sync.dma_start(out=v_words[:].bitcast(I32), in_=vals_words[0].bitcast(I32))
         nc.sync.dma_start(out=delta_sb[:], in_=delta)
 
-        def to_plane(picked, plane):
-            for quad in range(0, P, 32):
-                nc.sync.dma_start(out=plane[quad:quad + 4, :].bitcast(I32),
-                                  in_=picked[quad:quad + 32:SPREAD, :].bitcast(I32))
-
-        def gather(name, window, dtype, first, count, slot=None):
-            picked = tile(name, [P, count], dtype, slot)
-            nc.vector.tensor_copy(
-                out=picked[:], in_=window[:].indirect(slots[:, first // 16:(first + count) // 16]))
+        def gather(name, window, dtype, first, count, reuse=None):
+            picked = tile(name, [P, count], dtype, reuse)
+            entries = slots[:, first // LIST_ROWS:(first + count) // LIST_ROWS]
+            nc.vector.tensor_copy(out=picked[:], in_=window[:].indirect(entries))
             return picked
+
+        def to_plane(picked, plane):
+            for start in range(0, P, QUADRANT):
+                nc.sync.dma_start(out=plane[start:start + QUADRANT_BLOCKS, :].bitcast(I32),
+                                  in_=picked[start:start + QUADRANT:SPREAD, :].bitcast(I32))
 
         def interleave(name, raw):
             grouped = tile(name, [P, Q, PACK], BF16)
             nc.scalar.copy(out=grouped[:], in_=raw[:].rearrange("p j q -> p q j"))
             return grouped
 
-        def quantize(name, grouped, slot=None):
-            codes = tile(name + "_codes", [P, Q], U32, slot)
-            scales = tile(name + "_scales", [P, Q], U8)
-            nc.vector.quantize_mx(out=codes[:].bitcast(FP8X4), scales=scales[:],
+        def quantize(name, grouped):
+            codes = tile(name + "_codes", [P, Q], U32)
+            plane = tile(name + "_scales", [P, Q], U8)
+            nc.vector.quantize_mx(out=codes[:].bitcast(FP8X4), scales=plane[:],
                                   in_=grouped[:].rearrange("p q j -> p (q j)"))
-            return codes, scales
+            return codes, plane
 
-        def product(name, rows, words, scales):
+        def product(name, rows, words, plane, h):
+            row_codes, row_plane = rows
             acc = ps.tile([P, HALF], F32, name=name)
-            nc.tensor.matmul_mx(out=acc[:], lhsT=rows[0][:].bitcast(FP8X4), lhsT_scale=rows[1][:],
-                                rhs=words.bitcast(FP4X4), rhs_scale=scales, start=True, stop=True)
+            nc.tensor.matmul_mx(out=acc[:], lhsT=row_codes[:].bitcast(FP8X4), lhsT_scale=row_plane[:],
+                                rhs=words[:].bitcast(FP4X4), rhs_scale=plane[:, h * HALF:(h + 1) * HALF],
+                                start=True, stop=True)
             return acc
 
-        def weights(w, acc, bias, h):
-            for g in range(G // 2):
-                page = h * G // 2 + g
-                nc.scalar.activation(out=w[:, page * PAGE:(page + 1) * PAGE], in_=acc[:, g * PAGE:(g + 1) * PAGE],
+        def weights(w, scores, bias, h):
+            for n in range(G // 2):
+                page = h * G // 2 + n
+                nc.scalar.activation(out=w[:, page * PAGE:(page + 1) * PAGE],
+                                     in_=scores[:, n * PAGE:(n + 1) * PAGE],
                                      func=ACT.Exp, bias=bias[:, page:page + 1])
 
-        q_grouped = interleave("q_grouped", q_raw)
-        q_mx = quantize("q", q_grouped)
-        ks = gather("ks", k_bytes, U8, 0, I)
-        to_plane(ks, k_plane)
+        q_mx = quantize("q", interleave("q_grouped", q_raw))
+        to_plane(gather("ks", k_bytes, U8, 0, I), k_plane)
         kw0 = gather("kw0", k_words, U16, 0, HALF)
         picked_prior = tile("picked_prior", [P, G], F32)
         nc.vector.tensor_copy(out=picked_prior[:], in_=prior_sb[:].indirect(pages[:]))
-        a0 = product("a0", q_mx, kw0[:], k_plane[:, :HALF])
+        a0 = product("a0", q_mx, kw0, k_plane, 0)
 
         neg_lse = tile("neg_lse", [P, 1], F32)
         nc.scalar.mul(neg_lse[:], lse_sb[:], -1.0)
@@ -129,27 +135,36 @@ def tile_attend_gpagebias_kernel(tc, query, keys_words, keys_scales, gout, vals_
 
         to_plane(gather("vs", v_bytes, U8, 0, I), v_plane)
         g_mx = quantize("g", g_grouped)
-        kw1 = gather("kw1", k_words, U16, HALF, HALF, "g_raw")
-        a1 = product("a1", q_mx, kw1[:], k_plane[:, HALF:])
+        kw1 = gather("kw1", k_words, U16, HALF, HALF, reuse="g_raw")
+        a1 = product("a1", q_mx, kw1, k_plane, 1)
         weights(w, a1, bias, 1)
-        old_sb = tile("old_sb", [P, U], F32, "k_words")
+        old_sb = tile("old_sb", [P, U], F32, reuse="k_words")
         nc.sync.dma_start(out=old_sb[:], in_=old)
-        vw0 = gather("vw0", v_words, U16, 0, HALF)
-        dp0 = product("dp0", g_mx, vw0[:], v_plane[:, :HALF])
-        vw1 = gather("vw1", v_words, U16, HALF, HALF)
-        dp1 = product("dp1", g_mx, vw1[:], v_plane[:, HALF:])
+        dp0 = product("dp0", g_mx, gather("vw0", v_words, U16, 0, HALF), v_plane, 0)
+        dp1 = product("dp1", g_mx, gather("vw1", v_words, U16, HALF, HALF), v_plane, 1)
 
-        ds = []
-        for h, dp in enumerate((dp0, dp1)):
-            d = tile("ds%d" % h, [P, HALF], F32)
-            nc.vector.scalar_tensor_tensor(out=d[:], in0=dp[:], scalar=delta_sb[:], in1=w[:, h * HALF:(h + 1) * HALF],
+        sums = tile("sums", [P, G], F32)
+
+        def score_grads(ds, dp, h, cols):
+            nc.vector.scalar_tensor_tensor(out=ds[:, cols], in0=dp[:, cols], scalar=delta_sb[:],
+                                           in1=w[:, h * HALF + cols.start:h * HALF + cols.stop],
                                            op0=ALU.subtract, op1=ALU.mult)
-            ds.append(d)
-        sums = tile("sums", [P, G], F32, "w")
-        for h in range(2):
-            nc.vector.tensor_reduce(out=sums[:, h * G // 2:(h + 1) * G // 2],
-                                    in_=ds[h][:].rearrange("p (g j) -> p g j", j=PAGE),
+
+        def page_sums(ds, h, cols):
+            nc.vector.tensor_reduce(out=sums[:, (h * HALF + cols.start) // PAGE:(h * HALF + cols.stop) // PAGE],
+                                    in_=ds[:, cols].rearrange("p (g j) -> p g j", j=PAGE),
                                     axis=mybir.AxisListType.X, op=ALU.add)
+
+        ds0 = tile("ds0", [P, HALF], F32)
+        score_grads(ds0, dp0, 0, slice(0, HALF))
+        page_sums(ds0, 0, slice(0, HALF))
+        ds1 = tile("ds1", [P, HALF], F32, reuse="bias")
+        pieces = (slice(0, HALF // 2), slice(HALF // 2, HALF))
+        for cols in pieces:
+            score_grads(ds1, dp1, 1, cols)
+        for cols in pieces:
+            page_sums(ds1, 1, cols)
+
         nc.vector.tensor_tensor(out=fresh[:].indirect(pages[:]), in0=sums[:], in1=factor[:], op=ALU.mult)
         for c, queue in enumerate((nc.sync, nc.scalar)):
             cols = slice(c * U // 2, (c + 1) * U // 2)

from contextlib import ExitStack

import concourse.mybir as mybir

D, E, T, I, G, U, Q = 512, 512, 4096, 1024, 64, 512, 128
FLOPS = 2 * D * Q * I + 2 * E * Q * I

F32 = mybir.dt.float32
BF16 = mybir.dt.bfloat16
I32 = mybir.dt.int32
U32 = mybir.dt.uint32
U16 = mybir.dt.uint16
U8 = mybir.dt.uint8
FP8X4 = mybir.dt.float8_e4m3fn_x4
FP4X4 = mybir.dt.float4_e2m1fn_x4
ALU = mybir.AluOpType
ACT = mybir.ActivationFunctionType

P = 128
PACK = 4
QUADRANT = 32
QUADRANT_BLOCKS = 4
SPREAD = QUADRANT // QUADRANT_BLOCKS
LIST_ROWS = 16
PAGE = I // G
HALF = I // 2
LOSS_SCALE = 512.0


def tile_attend_gpagebias_kernel(tc, query, keys_words, keys_scales, gout, vals_words, vals_scales,
                                  lse, delta, prior, trust, old, offs, offs2, out):
    nc = tc.nc
    with ExitStack() as ctx:
        sb = ctx.enter_context(tc.tile_pool(name="sb", bufs=1))
        ps = ctx.enter_context(tc.psum_pool(name="ps", bufs=1))

        def tile(name, shape, dtype, reuse=None):
            return sb.tile(shape, dtype, name=name, tag=reuse or name, align_bytes=64)

        slots = sb.tile([P, I // LIST_ROWS], U16, name="slots")
        pages = sb.tile([P, G // LIST_ROWS], U16, name="pages")
        k_words = tile("k_words", [P, T], U16)
        k_bytes = tile("k_bytes", [P, T], U8)
        v_bytes = tile("v_bytes", [P, T], U8)
        q_raw = tile("q_raw", [P, PACK, Q], F32)
        prior_sb = tile("prior_sb", [P, U], F32)
        lse_sb = tile("lse_sb", [P, 1], F32)
        delta_sb = tile("delta_sb", [P, 1], F32)
        trust_sb = tile("trust_sb", [P, 1], F32)
        fresh = tile("fresh", [P, U], F32)
        loss = tile("loss", [P, G], F32)
        k_plane = tile("k_plane", [P, I], U8)
        v_plane = tile("v_plane", [P, I], U8)
        g_raw = tile("g_raw", [P, PACK, Q], F32)
        v_words = tile("v_words", [P, T], U16)
        ones = tile("ones", [P, G], F32)

        nc.gpsimd.memset(ones[:], 1.0)
        nc.scalar.mul(loss[:], ones[:], LOSS_SCALE)

        nc.vector.memset(k_bytes[:].bitcast(I32), 0)
        nc.vector.memset(v_bytes[:].bitcast(I32), 0)
        nc.vector.memset(k_plane[:].bitcast(I32), 0)
        nc.vector.memset(v_plane[:].bitcast(I32), 0)
        nc.vector.memset(fresh[:], 0.0)

        nc.sync.dma_start(slots[:], offs)
        nc.sync.dma_start(out=q_raw[:], in_=query.rearrange("(p j) q -> p j q", j=PACK))
        nc.sync.dma_start(out=prior_sb[:], in_=prior)
        nc.sync.dma_start(out=k_bytes[0:P:SPREAD, :].bitcast(I32), in_=keys_scales[0].bitcast(I32))
        nc.sync.dma_start(out=k_words[:].bitcast(I32), in_=keys_words[0].bitcast(I32))
        nc.sync.dma_start(pages[:], offs2)
        nc.sync.dma_start(out=trust_sb[:], in_=trust)
        nc.sync.dma_start(out=lse_sb[:], in_=lse)
        nc.sync.dma_start(out=v_bytes[0:P:SPREAD, :].bitcast(I32), in_=vals_scales[0].bitcast(I32))
        nc.sync.dma_start(out=g_raw[:], in_=gout.rearrange("(p j) q -> p j q", j=PACK))
        nc.sync.dma_start(out=v_words[:].bitcast(I32), in_=vals_words[0].bitcast(I32))
        nc.sync.dma_start(out=delta_sb[:], in_=delta)

        def gather(name, window, dtype, first, count, reuse=None):
            picked = tile(name, [P, count], dtype, reuse)
            entries = slots[:, first // LIST_ROWS:(first + count) // LIST_ROWS]
            nc.vector.tensor_copy(out=picked[:], in_=window[:].indirect(entries))
            return picked

        def to_plane(picked, plane):
            for start in range(0, P, QUADRANT):
                nc.sync.dma_start(out=plane[start:start + QUADRANT_BLOCKS, :].bitcast(I32),
                                  in_=picked[start:start + QUADRANT:SPREAD, :].bitcast(I32))

        def interleave(name, raw):
            grouped = tile(name, [P, Q, PACK], BF16)
            nc.scalar.copy(out=grouped[:], in_=raw[:].rearrange("p j q -> p q j"))
            return grouped

        def quantize(name, grouped):
            codes = tile(name + "_codes", [P, Q], U32)
            plane = tile(name + "_scales", [P, Q], U8)
            nc.vector.quantize_mx(out=codes[:].bitcast(FP8X4), scales=plane[:],
                                  in_=grouped[:].rearrange("p q j -> p (q j)"))
            return codes, plane

        def product(name, rows, words, plane, h):
            row_codes, row_plane = rows
            acc = ps.tile([P, HALF], F32, name=name)
            nc.tensor.matmul_mx(out=acc[:], lhsT=row_codes[:].bitcast(FP8X4), lhsT_scale=row_plane[:],
                                rhs=words[:].bitcast(FP4X4), rhs_scale=plane[:, h * HALF:(h + 1) * HALF],
                                start=True, stop=True)
            return acc

        def weights(w, scores, bias, h):
            for n in range(G // 2):
                page = h * G // 2 + n
                nc.scalar.activation(out=w[:, page * PAGE:(page + 1) * PAGE],
                                     in_=scores[:, n * PAGE:(n + 1) * PAGE],
                                     func=ACT.Exp, bias=bias[:, page:page + 1])

        q_mx = quantize("q", interleave("q_grouped", q_raw))
        to_plane(gather("ks", k_bytes, U8, 0, I), k_plane)
        kw0 = gather("kw0", k_words, U16, 0, HALF)
        picked_prior = tile("picked_prior", [P, G], F32)
        nc.vector.tensor_copy(out=picked_prior[:], in_=prior_sb[:].indirect(pages[:]))
        a0 = product("a0", q_mx, kw0, k_plane, 0)

        neg_lse = tile("neg_lse", [P, 1], F32)
        nc.scalar.mul(neg_lse[:], lse_sb[:], -1.0)
        factor = tile("factor", [P, G], F32)
        nc.scalar.activation(out=factor[:], in_=loss[:], func=ACT.Copy, scale=trust_sb[:])
        bias = tile("bias", [P, G], F32)
        nc.scalar.activation(out=bias[:], in_=picked_prior[:], func=ACT.Identity, scale=trust_sb[:],
                             bias=neg_lse[:])
        g_grouped = interleave("g_grouped", g_raw)
        w = tile("w", [P, I], F32)
        weights(w, a0, bias, 0)

        to_plane(gather("vs", v_bytes, U8, 0, I), v_plane)
        g_mx = quantize("g", g_grouped)
        kw1 = gather("kw1", k_words, U16, HALF, HALF, reuse="g_raw")
        a1 = product("a1", q_mx, kw1, k_plane, 1)
        weights(w, a1, bias, 1)
        old_sb = tile("old_sb", [P, U], F32, reuse="k_words")
        nc.sync.dma_start(out=old_sb[:], in_=old)
        dp0 = product("dp0", g_mx, gather("vw0", v_words, U16, 0, HALF), v_plane, 0)
        dp1 = product("dp1", g_mx, gather("vw1", v_words, U16, HALF, HALF), v_plane, 1)

        sums = tile("sums", [P, G], F32)

        def score_grads(ds, dp, h, cols):
            nc.vector.scalar_tensor_tensor(out=ds[:, cols], in0=dp[:, cols], scalar=delta_sb[:],
                                           in1=w[:, h * HALF + cols.start:h * HALF + cols.stop],
                                           op0=ALU.subtract, op1=ALU.mult)

        def page_sums(ds, h, cols):
            nc.vector.tensor_reduce(out=sums[:, (h * HALF + cols.start) // PAGE:(h * HALF + cols.stop) // PAGE],
                                    in_=ds[:, cols].rearrange("p (g j) -> p g j", j=PAGE),
                                    axis=mybir.AxisListType.X, op=ALU.add)

        ds0 = tile("ds0", [P, HALF], F32)
        score_grads(ds0, dp0, 0, slice(0, HALF))
        page_sums(ds0, 0, slice(0, HALF))
        ds1 = tile("ds1", [P, HALF], F32, reuse="bias")
        pieces = (slice(0, HALF // 2), slice(HALF // 2, HALF))
        for cols in pieces:
            score_grads(ds1, dp1, 1, cols)
        for cols in pieces:
            page_sums(ds1, 1, cols)

        nc.vector.tensor_tensor(out=fresh[:].indirect(pages[:]), in0=sums[:], in1=factor[:], op=ALU.mult)
        for c, queue in enumerate((nc.sync, nc.scalar)):
            cols = slice(c * U // 2, (c + 1) * U // 2)
            result = tile("result%d" % c, [P, U // 2], F32)
            nc.vector.tensor_tensor(out=result[:], in0=old_sb[:, cols], in1=fresh[:, cols], op=ALU.add)
            queue.dma_start(out=out[:, cols], in_=result[:])
